import numpy as np
import ml_dtypes


def mxq(x, axis, fmt="e4m3"):
    dtype, down = {"e4m3": (ml_dtypes.float8_e4m3fn, 7), "e5m2": (ml_dtypes.float8_e5m2, 14)}[fmt]
    v = np.moveaxis(np.asarray(x, np.float32).astype(ml_dtypes.bfloat16).astype(np.float64), axis, -1)
    blocks = v.reshape(v.shape[:-1] + (-1, 32))
    amax = np.abs(blocks).max(-1, keepdims=True)
    byte = np.maximum(np.where(amax > 0, np.frexp(amax)[1] - 1 + 127, 0) - down, 1)
    scale = np.exp2(byte - 127.0)
    codes = (blocks / scale).astype(np.float32).astype(dtype).astype(np.float64)
    return np.moveaxis((codes * scale).reshape(v.shape), -1, axis)


WIDE = False


def mx_kscale(k):
    if not WIDE:
        return np.ones(k)
    levels = np.array([10, -10, 5, -5, 0])
    if k % 512:
        return np.exp2(np.random.permutation(np.resize(levels, k // 32))).repeat(32)
    a = np.empty((k // 512, 16))
    for p in range(k // 512):
        a[p, :8] = np.random.permutation(np.resize(levels, 8))
        for g in range(8):
            far = levels[np.abs(levels - a[p, g]) >= 10]
            a[p, g + 8] = far[np.random.randint(len(far))]
    return np.exp2(a.ravel()).repeat(32)


def f64(x):
    return np.asarray(x).astype(np.float64)


def striped(idx):
    return np.tile(idx.reshape(-1, 16).T, (8, 1)).astype(np.uint16)


def unstriped(offs):
    return offs[:16].T.reshape(-1).astype(np.int64)


def pack_weight(w):
    k, n = w.shape
    w = f64(np.asarray(w, np.float32).astype(ml_dtypes.bfloat16)).reshape(k // 32, 32, n)
    amax = np.abs(w).max(1)
    byte = np.clip(np.where(amax > 0, np.frexp(amax)[1] - 1 + 127 - 7, 1), 1, 254)
    scaled = (w * np.exp2(127.0 - byte)[:, None, :]).reshape(k, n).astype(np.float32)
    words = np.ascontiguousarray(scaled.reshape(k // 512, 128, 4, n).transpose(0, 1, 3, 2)).astype(ml_dtypes.float8_e4m3fn).view(np.uint8)
    return words, np.ascontiguousarray(byte.astype(np.uint8).reshape(k // 512, 16, n))


def unpack_weight(words, scales):
    g, p, n, _ = words.shape
    vals = np.ascontiguousarray(words).view(ml_dtypes.float8_e4m3fn).astype(np.float64) * np.repeat(np.exp2(scales.astype(np.float64) - 127.0), 8, axis=1)[..., None]
    return vals.transpose(0, 1, 3, 2).reshape(g * 512, n)


H, K, T, S, N = 512, 512, 4096, 1024, 128


def setup_inputs():
    n = np.random.standard_normal
    s = mx_kscale(K)[:, None]
    u = mx_kscale(H)
    packed_xT = pack_weight(n((K, T)) * s)
    return {
        "x_words": packed_xT[0],
        "x_scales": packed_xT[1],
        "w1": (n((K, H)) / np.sqrt(K) / s).astype(np.float32),
        "unit": (np.random.uniform(0.5, 1.5, (H, 1)) * u[:, None]).astype(np.float32),
        "wo": (n((H, N)) / np.sqrt(H) / u[:, None]).astype(np.float32),
        "skip": (n((N, S))).astype(np.float32),
        "offs": striped(np.random.permutation(T)[:S]),
    }


def reference(x_words, x_scales, w1, unit, wo, skip, offs):
    xq = unpack_weight(x_words, x_scales)[:, unstriped(offs)]
    y = mxq(f64(w1), 0, "e4m3").T @ xq
    lum = np.exp(y)
    lmean = y.mean(axis=1, keepdims=True)
    key = np.exp(lmean)
    sc = 0.8 * (lum / key)
    tm = (sc * (0.15 * sc + 1.0)) / (sc + 1.0)
    zz = f64(unit) * tm
    return (mxq(f64(wo), 0, "e4m3").T @ mxq(zz, 0, "e4m3")) + f64(skip)

@@ -1,0 +1,209 @@
+import math
+from contextlib import ExitStack
+
+import concourse.mybir as mybir
+
+H, K, T, S, N = 512, 512, 4096, 1024, 128
+FLOPS = 2 * K * H * S + 2 * H * N * S
+
+F32 = mybir.dt.float32
+BF16 = mybir.dt.bfloat16
+I32 = mybir.dt.int32
+U32 = mybir.dt.uint32
+U16 = mybir.dt.uint16
+U8 = mybir.dt.uint8
+FP8X4 = mybir.dt.float8_e4m3fn_x4
+ALU = mybir.AluOpType
+ACT = mybir.ActivationFunctionType
+
+P = 128
+PACK = 4
+HALF = 512
+CHUNKS = (512, 256, 128, 128)
+SCALAR_SUMS = ((0, 0), (1, 0))
+LEAD = 1024
+Y_SCALE = 1.0 / (2 * S)
+
+
+def tile_picked_ytonem_global_p_kernel(
+    tc, x_words, x_scales, w1, unit, wo, skip, offs, out
+):
+    nc = tc.nc
+    with ExitStack() as ctx:
+        keep = ctx.enter_context(tc.tile_pool(name="keep", bufs=1))
+        psum = ctx.enter_context(tc.psum_pool(name="psum", bufs=1))
+
+        def tile(shape, dtype, name):
+            return keep.tile(shape, dtype, name=name, align_bytes=64)
+
+        offsets = keep.tile([P, S // 16], U16, name="offsets")
+        nc.sync.dma_start(offsets[:], offs)
+        unit_sb = tile([P, PACK], F32, "unit_sb")
+        nc.sync.dma_start(unit_sb[:], unit.rearrange("(p t) o -> p (t o)", t=PACK))
+        scale_rows = tile([P, T], U8, "scale_rows")
+        nc.vector.memset(scale_rows[:].bitcast(I32), 0)
+        words = tile([P, T], I32, "words")
+        x_rows = x_words[0].rearrange("p n t -> p (n t)").bitcast(I32)
+        nc.sync.dma_start(words[:, 0:LEAD], x_rows[:, 0:LEAD])
+        nc.sync.dma_start(scale_rows[0:P:8, :].bitcast(I32), x_scales[0].bitcast(I32))
+        nc.sync.dma_start(words[:, LEAD:T], x_rows[:, LEAD:T])
+        w1_raw = tile([P, PACK, H], F32, "w1_raw")
+        nc.sync.dma_start(w1_raw[:], w1.rearrange("(p j) c -> p j c", j=PACK))
+        x_plane = tile([P, S], U8, "x_plane")
+        nc.gpsimd.memset(x_plane[:], 0)
+
+        one = tile([P, 1], F32, "one")
+        nc.gpsimd.memset(one[:], 1.0)
+        ln_c = tile([P, 1], F32, "ln_c")
+        nc.scalar.activation(ln_c[:], one[:], ACT.Ln, scale=0.425)
+        twice = tile([P, PACK], F32, "twice")
+        nc.gpsimd.tensor_scalar(twice[:], unit_sb[:], 0.0, 2.0, ALU.is_ge, ALU.mult)
+        sgn = tile([P, PACK], F32, "sgn")
+        nc.gpsimd.tensor_scalar(sgn[:], twice[:], -1.0, 1.0, ALU.add, ALU.mult)
+        mag = tile([P, PACK], F32, "mag")
+        nc.gpsimd.tensor_tensor(mag[:], unit_sb[:], sgn[:], ALU.mult)
+        parts = tile([P, 3, PACK], F32, "parts")
+        nc.gpsimd.tensor_scalar(parts[:, 0, :], mag[:], 2.0**63, 2.0**-63, ALU.min, ALU.max)
+        nc.gpsimd.tensor_scalar(parts[:, 1, :], mag[:], 2.0**127, 2.0**63, ALU.min, ALU.max)
+        nc.gpsimd.tensor_scalar(parts[:, 2, :], mag[:], 2.0**-63, 2.0**-126, ALU.min, ALU.max)
+        logs = tile([P, 3, PACK], F32, "logs")
+        for part, back in enumerate((1.0, 2.0**-63, 2.0**63)):
+            nc.scalar.activation(logs[:, part, :], parts[:, part, :], ACT.Ln, scale=back)
+        inverse = tile([P, PACK], F32, "inverse")
+        nc.scalar.activation(inverse[:], logs[:, 0, :], ACT.Exp, scale=-1.0)
+        ratio = tile([P, PACK], F32, "ratio")
+        nc.gpsimd.tensor_tensor(ratio[:], parts[:, 0, :], inverse[:], ALU.mult)
+        fix = tile([P, PACK], F32, "fix")
+        nc.gpsimd.tensor_scalar(fix[:], ratio[:], -1.0, ln_c[:], ALU.add, ALU.add)
+        outer = tile([P, PACK], F32, "outer")
+        nc.gpsimd.tensor_tensor(outer[:], logs[:, 1, :], logs[:, 2, :], ALU.add)
+        fixed = tile([P, PACK], F32, "fixed")
+        nc.gpsimd.tensor_tensor(fixed[:], fix[:], outer[:], ALU.add)
+        ln_unit = tile([P, PACK], F32, "ln_unit")
+        nc.gpsimd.tensor_tensor(ln_unit[:], fixed[:], logs[:, 0, :], ALU.add)
+
+        picked_rows = keep.tile([P, S], U8, name="picked_rows", tag="late", align_bytes=64)
+        nc.vector.tensor_copy(picked_rows[:], scale_rows[:].indirect(offsets[:]))
+        for q in range(4):
+            nc.scalar.dma_start(
+                x_plane[32 * q : 32 * q + 4, :].bitcast(I32),
+                picked_rows[32 * q : 32 * q + 32 : 8, :].bitcast(I32),
+            )
+        late = keep.tile([P, PACK * N + S], F32, name="late", tag="late", align_bytes=64)
+        wo_raw = late[:, 0 : PACK * N]
+        skip_sb = late[:, PACK * N : PACK * N + S]
+        nc.sync.dma_start(wo_raw, wo.rearrange("(p j) m -> p (j m)", j=PACK))
+        nc.sync.dma_start(skip_sb, skip)
+        x_codes = []
+        for h in range(2):
+            picked = tile([P, HALF], U32, "picked%d" % h)
+            nc.vector.tensor_copy(
+                picked[:], words[:].bitcast(U32).indirect(offsets[:, h * 32 : (h + 1) * 32])
+            )
+            x_codes.append(picked)
+
+        w1_src = w1_raw[:].rearrange("p j (m t) -> p m j t", t=PACK)
+        w1_codes, w1_planes = [], []
+        grouped = [tile([P, 2, P, PACK], BF16, "w1_grouped%d" % u) for u in range(2)]
+        nc.vector.tensor_copy(grouped[0][:].rearrange("p t m j -> p m j t"), w1_src[:, :, :, 0:2])
+        nc.scalar.copy(grouped[1][:].rearrange("p t m j -> p m j t"), w1_src[:, :, :, 2:4])
+        for t in range(PACK):
+            codes = tile([P, P], U32, "w1_codes%d" % t)
+            plane = tile([P, P], U8, "w1_plane%d" % t)
+            nc.vector.quantize_mx(
+                out=codes[:].bitcast(FP8X4),
+                scales=plane[:],
+                in_=grouped[t // 2][:, t % 2, :, :].rearrange("p m j -> p (m j)"),
+            )
+            w1_codes.append(codes)
+            w1_planes.append(plane)
+
+        half_ln = -0.5 * math.log(0.8)
+        ys, tanh_bias, exp_bias = [], [], []
+        for t in range(PACK):
+            y = tile([P, S], F32, "y%d" % t)
+            start = half_ln
+            for h in range(2):
+                cols = slice(h * HALF, (h + 1) * HALF)
+                bank = psum.tile([P, HALF], F32, name="bank%d" % (2 * t + h))
+                nc.tensor.matmul_mx(
+                    out=bank[:],
+                    lhsT=w1_codes[t][:].bitcast(FP8X4),
+                    lhsT_scale=w1_planes[t][:],
+                    rhs=x_codes[h][:].bitcast(FP8X4),
+                    rhs_scale=x_plane[:, cols],
+                    start=True,
+                    stop=True,
+                )
+                total = tile([P, 1], F32, "total%d_%d" % (t, h))
+                if (t, h) in SCALAR_SUMS:
+                    bare = tile([P, 1], F32, "bare%d" % t)
+                    nc.scalar.activation(y[:, cols], bank[:], ACT.Copy, scale=Y_SCALE, accum_out=bare[:])
+                    nc.scalar.activation(total[:], bare[:], ACT.Copy, bias=start)
+                else:
+                    nc.vector.tensor_scalar(
+                        y[:, cols], bank[:], Y_SCALE, start, ALU.mult, ALU.add, accum_out=total[:]
+                    )
+                start = total[:]
+            bias = tile([P, 1], F32, "exp_bias%d" % t)
+            nc.vector.tensor_scalar(bias[:], start, -2.0, ln_unit[:, t : t + 1], ALU.mult, ALU.add)
+            ys.append(y)
+            tanh_bias.append(start)
+            exp_bias.append(bias[:])
+
+        wo_grouped = tile([P, N, PACK], BF16, "wo_grouped")
+        nc.gpsimd.tensor_tensor(
+            wo_grouped[:].rearrange("p (c i) j -> p c j i", i=4),
+            wo_raw.rearrange("p (j c i) -> p c j i", j=PACK, i=4),
+            sgn[:].unsqueeze(1).unsqueeze(3).to_broadcast([P, N // 4, PACK, 4]),
+            ALU.mult,
+        )
+        wo_codes = tile([P, N], U32, "wo_codes")
+        wo_plane = tile([P, N], U8, "wo_plane")
+        nc.vector.quantize_mx(
+            out=wo_codes[:].bitcast(FP8X4), scales=wo_plane[:], in_=wo_grouped[:].rearrange("p m j -> p (m j)")
+        )
+
+        first = 0
+        for c, width in enumerate(CHUNKS):
+            cols = slice(first, first + width)
+            first += width
+            runs = width // 4
+            th = tile([P, runs, PACK, 4], F32, "th%d" % c)
+            ex = tile([P, runs, PACK, 4], F32, "ex%d" % c)
+            for t in range(PACK):
+                src = ys[t][:, cols].rearrange("p (r i) -> p r i", i=4)
+                nc.scalar.activation(th[:, :, t, :], src, ACT.Tanh, bias=tanh_bias[t], scale=-0.5 / Y_SCALE)
+                nc.scalar.activation(ex[:, :, t, :], src, ACT.Exp, bias=exp_bias[t], scale=1.0 / Y_SCALE)
+            zz = tile([P, 4, runs, PACK], BF16, "zz%d" % c)
+            nc.vector.scalar_tensor_tensor(
+                zz[:].rearrange("p i r t -> p (r t) i"),
+                th[:].rearrange("p r t i -> p (r t) i"),
+                0.575 / 0.425,
+                ex[:].rearrange("p r t i -> p (r t) i"),
+                ALU.add,
+                ALU.mult,
+            )
+            zz_codes = tile([P, width], U32, "zz_codes%d" % c)
+            zz_plane = tile([P, width], U8, "zz_plane%d" % c)
+            nc.vector.quantize_mx(
+                out=zz_codes[:].bitcast(FP8X4), scales=zz_plane[:], in_=zz[:].rearrange("p i r t -> p (i r t)")
+            )
+            acc = psum.tile([P, HALF], F32, name="bank%d" % c)
+            nc.tensor.matmul_mx(
+                out=acc[:, 0:width],
+                lhsT=wo_codes[:].bitcast(FP8X4),
+                lhsT_scale=wo_plane[:],
+                rhs=zz_codes[:].bitcast(FP8X4),
+                rhs_scale=zz_plane[:],
+                start=True,
+                stop=True,
+            )
+            result = tile([P, width], F32, "result%d" % c)
+            nc.vector.tensor_tensor(
+                result[:].rearrange("p (r i) -> p r i", i=4),
+                acc[:, 0:width].rearrange("p (i r) -> p r i", i=4),
+                skip_sb[:, cols].rearrange("p (r i) -> p r i", i=4),
+                ALU.add,
+            )
+            nc.sync.dma_start(out[:, cols], result[:])

@@ -19,9 +19,11 @@ ACT = mybir.ActivationFunctionType
 P = 128
 PACK = 4
 HALF = 512
-CHUNKS = (512, 256, 128, 128)
-SCALAR_SUMS = ((0, 0), (1, 0))
-LEAD = 1024
+CHUNKS = ((256,), (256,), (128, 64), (128,), (128,), (64,))
+LEADS = (512, 512, 256, 256)
+SCALAR_SUMS = (0, 2)
+FOLD = 128
+FOLDED = 1
 Y_SCALE = 1.0 / (2 * S)
 
 
@@ -37,35 +39,35 @@ def tile_picked_ytonem_global_p_kernel(
             return keep.tile(shape, dtype, name=name, align_bytes=64)
 
         offsets = keep.tile([P, S // 16], U16, name="offsets")
-        nc.sync.dma_start(offsets[:], offs)
         unit_sb = tile([P, PACK], F32, "unit_sb")
-        nc.sync.dma_start(unit_sb[:], unit.rearrange("(p t) o -> p (t o)", t=PACK))
+        nc.scalar.dma_start(unit_sb[:], unit.rearrange("(p t) o -> p (t o)", t=PACK))
         scale_rows = tile([P, T], U8, "scale_rows")
         nc.vector.memset(scale_rows[:].bitcast(I32), 0)
-        words = tile([P, T], I32, "words")
-        x_rows = x_words[0].rearrange("p n t -> p (n t)").bitcast(I32)
-        nc.sync.dma_start(words[:, 0:LEAD], x_rows[:, 0:LEAD])
-        nc.sync.dma_start(scale_rows[0:P:8, :].bitcast(I32), x_scales[0].bitcast(I32))
-        nc.sync.dma_start(words[:, LEAD:T], x_rows[:, LEAD:T])
         w1_raw = tile([P, PACK, H], F32, "w1_raw")
-        nc.sync.dma_start(w1_raw[:], w1.rearrange("(p j) c -> p j c", j=PACK))
+        w1_rows = w1.rearrange("(p j) c -> p j c", j=PACK)
+        nc.sync.dma_start(w1_raw[:, 0:2, :], w1_rows[:, 0:2, :])
+        nc.sync.dma_start(offsets[:], offs)
+        nc.sync.dma_start(scale_rows[0:P:8, :].bitcast(I32), x_scales[0].bitcast(I32))
+        nc.sync.dma_start(w1_raw[:, 2:4, :], w1_rows[:, 2:4, :])
+        words = tile([P, T], I32, "words")
+        nc.sync.dma_start(words[:], x_words[0].rearrange("p n t -> p (n t)").bitcast(I32))
         x_plane = tile([P, S], U8, "x_plane")
-        nc.gpsimd.memset(x_plane[:], 0)
+        nc.vector.memset(x_plane[:].bitcast(I32), 0)
 
         one = tile([P, 1], F32, "one")
         nc.gpsimd.memset(one[:], 1.0)
         ln_c = tile([P, 1], F32, "ln_c")
         nc.scalar.activation(ln_c[:], one[:], ACT.Ln, scale=0.425)
         twice = tile([P, PACK], F32, "twice")
-        nc.gpsimd.tensor_scalar(twice[:], unit_sb[:], 0.0, 2.0, ALU.is_ge, ALU.mult)
+        nc.vector.tensor_scalar(twice[:], unit_sb[:], 0.0, 2.0, ALU.is_ge, ALU.mult)
         sgn = tile([P, PACK], F32, "sgn")
         nc.gpsimd.tensor_scalar(sgn[:], twice[:], -1.0, 1.0, ALU.add, ALU.mult)
         mag = tile([P, PACK], F32, "mag")
-        nc.gpsimd.tensor_tensor(mag[:], unit_sb[:], sgn[:], ALU.mult)
+        nc.vector.scalar_tensor_tensor(mag[:], unit_sb[:], -1.0, unit_sb[:], ALU.mult, ALU.max)
         parts = tile([P, 3, PACK], F32, "parts")
-        nc.gpsimd.tensor_scalar(parts[:, 0, :], mag[:], 2.0**63, 2.0**-63, ALU.min, ALU.max)
-        nc.gpsimd.tensor_scalar(parts[:, 1, :], mag[:], 2.0**127, 2.0**63, ALU.min, ALU.max)
-        nc.gpsimd.tensor_scalar(parts[:, 2, :], mag[:], 2.0**-63, 2.0**-126, ALU.min, ALU.max)
+        nc.vector.tensor_scalar(parts[:, 0, :], mag[:], 2.0**63, 2.0**-63, ALU.min, ALU.max)
+        nc.vector.tensor_scalar(parts[:, 1, :], mag[:], 2.0**127, 2.0**63, ALU.min, ALU.max)
+        nc.vector.tensor_scalar(parts[:, 2, :], mag[:], 2.0**-63, 2.0**-126, ALU.min, ALU.max)
         logs = tile([P, 3, PACK], F32, "logs")
         for part, back in enumerate((1.0, 2.0**-63, 2.0**63)):
             nc.scalar.activation(logs[:, part, :], parts[:, part, :], ACT.Ln, scale=back)
@@ -102,11 +104,11 @@ def tile_picked_ytonem_global_p_kernel(
             )
             x_codes.append(picked)
 
-        w1_src = w1_raw[:].rearrange("p j (m t) -> p m j t", t=PACK)
         w1_codes, w1_planes = [], []
         grouped = [tile([P, 2, P, PACK], BF16, "w1_grouped%d" % u) for u in range(2)]
-        nc.vector.tensor_copy(grouped[0][:].rearrange("p t m j -> p m j t"), w1_src[:, :, :, 0:2])
-        nc.scalar.copy(grouped[1][:].rearrange("p t m j -> p m j t"), w1_src[:, :, :, 2:4])
+        w1_src = w1_raw[:].rearrange("p j (m t) -> p m j t", t=PACK)
+        for u, copy in enumerate((nc.vector.tensor_copy, nc.scalar.copy)):
+            copy(grouped[u][:].rearrange("p t m j -> p m j t"), w1_src[:, :, :, 2 * u : 2 * u + 2])
         for t in range(PACK):
             codes = tile([P, P], U32, "w1_codes%d" % t)
             plane = tile([P, P], U8, "w1_plane%d" % t)
@@ -118,45 +120,83 @@ def tile_picked_ytonem_global_p_kernel(
             w1_codes.append(codes)
             w1_planes.append(plane)
 
-        half_ln = -0.5 * math.log(0.8)
-        ys, tanh_bias, exp_bias = [], [], []
-        for t in range(PACK):
-            y = tile([P, S], F32, "y%d" % t)
-            start = half_ln
-            for h in range(2):
-                cols = slice(h * HALF, (h + 1) * HALF)
-                bank = psum.tile([P, HALF], F32, name="bank%d" % (2 * t + h))
-                nc.tensor.matmul_mx(
-                    out=bank[:],
-                    lhsT=w1_codes[t][:].bitcast(FP8X4),
-                    lhsT_scale=w1_planes[t][:],
-                    rhs=x_codes[h][:].bitcast(FP8X4),
-                    rhs_scale=x_plane[:, cols],
-                    start=True,
-                    stop=True,
-                )
-                total = tile([P, 1], F32, "total%d_%d" % (t, h))
-                if (t, h) in SCALAR_SUMS:
-                    bare = tile([P, 1], F32, "bare%d" % t)
-                    nc.scalar.activation(y[:, cols], bank[:], ACT.Copy, scale=Y_SCALE, accum_out=bare[:])
-                    nc.scalar.activation(total[:], bare[:], ACT.Copy, bias=start)
-                else:
-                    nc.vector.tensor_scalar(
-                        y[:, cols], bank[:], Y_SCALE, start, ALU.mult, ALU.add, accum_out=total[:]
-                    )
-                start = total[:]
-            bias = tile([P, 1], F32, "exp_bias%d" % t)
-            nc.vector.tensor_scalar(bias[:], start, -2.0, ln_unit[:, t : t + 1], ALU.mult, ALU.add)
-            ys.append(y)
-            tanh_bias.append(start)
-            exp_bias.append(bias[:])
+        def product(dst, t, h, lo, hi, start, stop):
+            nc.tensor.matmul_mx(
+                out=dst,
+                lhsT=w1_codes[t][:].bitcast(FP8X4),
+                lhsT_scale=w1_planes[t][:],
+                rhs=x_codes[h][:, lo:hi].bitcast(FP8X4),
+                rhs_scale=x_plane[:, h * HALF + lo : h * HALF + hi],
+                start=start,
+                stop=stop,
+            )
 
+        half_ln = -0.5 * math.log(0.8)
+        biases = tile([P, 2, PACK], F32, "biases")
+        folded = psum.tile([P, HALF], F32, name="bank7")
+        summed = [t for t in range(PACK) if t != FOLDED]
+        ys = {t: tile([P, S], F32, "y%d" % t) for t in summed}
+        banks, totals = {}, {}
+
+        def whole_half(t, h):
+            banks[t, h] = psum.tile([P, HALF], F32, name="bank%d" % (2 * t + h))
+            product(banks[t, h][:], t, h, 0, HALF, True, True)
+
+        def fold_half(h):
+            for lo in range(0, HALF, FOLD):
+                product(folded[:, 0:FOLD], FOLDED, h, lo, lo + FOLD, (h, lo) == (0, 0), (h, lo) == (1, HALF - FOLD))
+
+        def exp_bias(t):
+            nc.vector.tensor_scalar(
+                biases[:, 1, t : t + 1], biases[:, 0, t : t + 1], -2.0, ln_unit[:, t : t + 1], ALU.mult, ALU.add
+            )
+
+        def first_half(t):
+            whole_half(t, 0)
+            totals[t] = tile([P, 1], F32, "total%d" % t)
+            if t in SCALAR_SUMS:
+                bare = tile([P, 1], F32, "bare%d" % t)
+                nc.scalar.activation(ys[t][:, 0:HALF], banks[t, 0][:], ACT.Copy, scale=Y_SCALE, accum_out=bare[:])
+                nc.scalar.activation(totals[t][:], bare[:], ACT.Copy, bias=half_ln)
+            else:
+                nc.vector.tensor_scalar(
+                    ys[t][:, 0:HALF], banks[t, 0][:], Y_SCALE, half_ln, ALU.mult, ALU.add, accum_out=totals[t][:]
+                )
+
+        def second_half(t):
+            whole_half(t, 1)
+            nc.vector.tensor_scalar(
+                ys[t][:, HALF:S], banks[t, 1][:], Y_SCALE, totals[t][:], ALU.mult, ALU.add,
+                accum_out=biases[:, 0, t : t + 1],
+            )
+            exp_bias(t)
+
+        first_half(0)
+        first_half(2)
+        second_half(0)
+        fold_half(0)
+        fold_half(1)
+        row_sum = tile([P, 1], F32, "row_sum")
+        nc.vector.tensor_reduce(row_sum[:], folded[:, 0:FOLD], mybir.AxisListType.X, ALU.add)
+        nc.vector.tensor_scalar(biases[:, 0, FOLDED : FOLDED + 1], row_sum[:], Y_SCALE, half_ln, ALU.mult, ALU.add)
+        exp_bias(FOLDED)
+        whole_half(FOLDED, 0)
+        first_half(3)
+        second_half(2)
+        second_half(3)
+        whole_half(FOLDED, 1)
+        late_biases = tile([P, 2, PACK], F32, "late_biases")
+        nc.vector.tensor_copy(late_biases[:], biases[:])
+
+        wo_signed = tile([P, PACK, N], BF16, "wo_signed")
+        for j in range(PACK):
+            nc.gpsimd.tensor_scalar(
+                wo_signed[:, j, :], wo_raw[:, j * N : (j + 1) * N], sgn[:, j : j + 1], 0.0, ALU.mult, ALU.add
+            )
         wo_grouped = tile([P, N, PACK], BF16, "wo_grouped")
-        nc.gpsimd.tensor_tensor(
+        nc.vector.tensor_copy(
             wo_grouped[:].rearrange("p (c i) j -> p c j i", i=4),
-            wo_raw.rearrange("p (j c i) -> p c j i", j=PACK, i=4),
-            sgn[:].unsqueeze(1).unsqueeze(3).to_broadcast([P, N // 4, PACK, 4]),
-            ALU.mult,
+            wo_signed[:].rearrange("p j (c i) -> p c j i", i=4),
         )
         wo_codes = tile([P, N], U32, "wo_codes")
         wo_plane = tile([P, N], U8, "wo_plane")
@@ -164,46 +204,74 @@ def tile_picked_ytonem_global_p_kernel(
             out=wo_codes[:].bitcast(FP8X4), scales=wo_plane[:], in_=wo_grouped[:].rearrange("p m j -> p (m j)")
         )
 
-        first = 0
-        for c, width in enumerate(CHUNKS):
-            cols = slice(first, first + width)
-            first += width
-            runs = width // 4
-            th = tile([P, runs, PACK, 4], F32, "th%d" % c)
-            ex = tile([P, runs, PACK, 4], F32, "ex%d" % c)
-            for t in range(PACK):
-                src = ys[t][:, cols].rearrange("p (r i) -> p r i", i=4)
-                nc.scalar.activation(th[:, :, t, :], src, ACT.Tanh, bias=tanh_bias[t], scale=-0.5 / Y_SCALE)
-                nc.scalar.activation(ex[:, :, t, :], src, ACT.Exp, bias=exp_bias[t], scale=1.0 / Y_SCALE)
-            zz = tile([P, 4, runs, PACK], BF16, "zz%d" % c)
+        th = tile([P, S // 4, PACK, 4], F32, "th")
+        ex = tile([P, S // 4, PACK, 4], F32, "ex")
+
+        def activate(t, a, b):
+            if t == FOLDED:
+                src, back = banks[t, a // HALF][:, a % HALF : a % HALF + b - a], 1.0
+            else:
+                src, back = ys[t][:, a:b], 1.0 / Y_SCALE
+            src = src.rearrange("p (r i) -> p r i", i=4)
+            rows = slice(a // 4, b // 4)
+            shifts = late_biases if a else biases
+            nc.scalar.activation(th[:, rows, t, :], src, ACT.Tanh, bias=shifts[:, 0, t : t + 1], scale=-0.5 * back)
+            nc.scalar.activation(ex[:, rows, t, :], src, ACT.Exp, bias=shifts[:, 1, t : t + 1], scale=back)
+
+        def combine(a, b):
+            rows = slice(a // 4, b // 4)
+            zz = tile([P, 4, (b - a) // 4, PACK], BF16, "zz%d" % a)
             nc.vector.scalar_tensor_tensor(
                 zz[:].rearrange("p i r t -> p (r t) i"),
-                th[:].rearrange("p r t i -> p (r t) i"),
+                th[:, rows, :, :].rearrange("p r t i -> p (r t) i"),
                 0.575 / 0.425,
-                ex[:].rearrange("p r t i -> p (r t) i"),
+                ex[:, rows, :, :].rearrange("p r t i -> p (r t) i"),
                 ALU.add,
                 ALU.mult,
             )
-            zz_codes = tile([P, width], U32, "zz_codes%d" % c)
-            zz_plane = tile([P, width], U8, "zz_plane%d" % c)
-            nc.vector.quantize_mx(
-                out=zz_codes[:].bitcast(FP8X4), scales=zz_plane[:], in_=zz[:].rearrange("p i r t -> p (i r t)")
-            )
-            acc = psum.tile([P, HALF], F32, name="bank%d" % c)
-            nc.tensor.matmul_mx(
-                out=acc[:, 0:width],
-                lhsT=wo_codes[:].bitcast(FP8X4),
-                lhsT_scale=wo_plane[:],
-                rhs=zz_codes[:].bitcast(FP8X4),
-                rhs_scale=zz_plane[:],
-                start=True,
-                stop=True,
-            )
-            result = tile([P, width], F32, "result%d" % c)
+            return zz[:].rearrange("p i r t -> p (i r t)")
+
+        free_banks = [0, 1, 4, 5, 6, 7]
+
+        def read_out(first, zz_flat, pieces):
+            acc = psum.tile([P, HALF], F32, name="bank%d" % free_banks.pop(0))
+            at = 0
+            for piece in pieces:
+                zz_codes = tile([P, piece], U32, "zz_codes%d" % (first + at))
+                zz_plane = tile([P, piece], U8, "zz_plane%d" % (first + at))
+                nc.vector.quantize_mx(
+                    out=zz_codes[:].bitcast(FP8X4),
+                    scales=zz_plane[:],
+                    in_=zz_flat[:, PACK * at : PACK * (at + piece)],
+                )
+                nc.tensor.matmul_mx(
+                    out=acc[:, at : at + piece],
+                    lhsT=wo_codes[:].bitcast(FP8X4),
+                    lhsT_scale=wo_plane[:],
+                    rhs=zz_codes[:].bitcast(FP8X4),
+                    rhs_scale=zz_plane[:],
+                    start=True,
+                    stop=True,
+                )
+                at += piece
+            cols = slice(first, first + at)
+            result = tile([P, at], F32, "result%d" % first)
             nc.vector.tensor_tensor(
                 result[:].rearrange("p (r i) -> p r i", i=4),
-                acc[:, 0:width].rearrange("p (i r) -> p r i", i=4),
+                acc[:, 0:at].rearrange("p (i r) -> p r i", i=4),
                 skip_sb[:, cols].rearrange("p (r i) -> p r i", i=4),
                 ALU.add,
             )
             nc.sync.dma_start(out[:, cols], result[:])
+
+        done = [0] * PACK
+        first = 0
+        for pieces in CHUNKS:
+            last = first + sum(pieces)
+            for t in range(PACK):
+                if done[t] < last:
+                    reach = max(last, LEADS[t])
+                    activate(t, done[t], reach)
+                    done[t] = reach
+            read_out(first, combine(first, last), pieces)
+            first = last

import math
from contextlib import ExitStack

import concourse.mybir as mybir

H, K, T, S, N = 512, 512, 4096, 1024, 128
FLOPS = 2 * K * H * S + 2 * H * N * S

F32 = mybir.dt.float32
BF16 = mybir.dt.bfloat16
I32 = mybir.dt.int32
U32 = mybir.dt.uint32
U16 = mybir.dt.uint16
U8 = mybir.dt.uint8
FP8X4 = mybir.dt.float8_e4m3fn_x4
ALU = mybir.AluOpType
ACT = mybir.ActivationFunctionType

P = 128
PACK = 4
HALF = 512
CHUNKS = ((256,), (256,), (128, 64), (128,), (128,), (64,))
LEADS = (512, 512, 256, 256)
SCALAR_SUMS = (0, 2)
FOLD = 128
FOLDED = 1
Y_SCALE = 1.0 / (2 * S)


def tile_picked_ytonem_global_p_kernel(
    tc, x_words, x_scales, w1, unit, wo, skip, offs, out
):
    nc = tc.nc
    with ExitStack() as ctx:
        keep = ctx.enter_context(tc.tile_pool(name="keep", bufs=1))
        psum = ctx.enter_context(tc.psum_pool(name="psum", bufs=1))

        def tile(shape, dtype, name):
            return keep.tile(shape, dtype, name=name, align_bytes=64)

        offsets = keep.tile([P, S // 16], U16, name="offsets")
        unit_sb = tile([P, PACK], F32, "unit_sb")
        nc.scalar.dma_start(unit_sb[:], unit.rearrange("(p t) o -> p (t o)", t=PACK))
        scale_rows = tile([P, T], U8, "scale_rows")
        nc.vector.memset(scale_rows[:].bitcast(I32), 0)
        w1_raw = tile([P, PACK, H], F32, "w1_raw")
        w1_rows = w1.rearrange("(p j) c -> p j c", j=PACK)
        nc.sync.dma_start(w1_raw[:, 0:2, :], w1_rows[:, 0:2, :])
        nc.sync.dma_start(offsets[:], offs)
        nc.sync.dma_start(scale_rows[0:P:8, :].bitcast(I32), x_scales[0].bitcast(I32))
        nc.sync.dma_start(w1_raw[:, 2:4, :], w1_rows[:, 2:4, :])
        words = tile([P, T], I32, "words")
        nc.sync.dma_start(words[:], x_words[0].rearrange("p n t -> p (n t)").bitcast(I32))
        x_plane = tile([P, S], U8, "x_plane")
        nc.vector.memset(x_plane[:].bitcast(I32), 0)

        one = tile([P, 1], F32, "one")
        nc.gpsimd.memset(one[:], 1.0)
        ln_c = tile([P, 1], F32, "ln_c")
        nc.scalar.activation(ln_c[:], one[:], ACT.Ln, scale=0.425)
        twice = tile([P, PACK], F32, "twice")
        nc.vector.tensor_scalar(twice[:], unit_sb[:], 0.0, 2.0, ALU.is_ge, ALU.mult)
        sgn = tile([P, PACK], F32, "sgn")
        nc.gpsimd.tensor_scalar(sgn[:], twice[:], -1.0, 1.0, ALU.add, ALU.mult)
        mag = tile([P, PACK], F32, "mag")
        nc.vector.scalar_tensor_tensor(mag[:], unit_sb[:], -1.0, unit_sb[:], ALU.mult, ALU.max)
        parts = tile([P, 3, PACK], F32, "parts")
        nc.vector.tensor_scalar(parts[:, 0, :], mag[:], 2.0**63, 2.0**-63, ALU.min, ALU.max)
        nc.vector.tensor_scalar(parts[:, 1, :], mag[:], 2.0**127, 2.0**63, ALU.min, ALU.max)
        nc.vector.tensor_scalar(parts[:, 2, :], mag[:], 2.0**-63, 2.0**-126, ALU.min, ALU.max)
        logs = tile([P, 3, PACK], F32, "logs")
        for part, back in enumerate((1.0, 2.0**-63, 2.0**63)):
            nc.scalar.activation(logs[:, part, :], parts[:, part, :], ACT.Ln, scale=back)
        inverse = tile([P, PACK], F32, "inverse")
        nc.scalar.activation(inverse[:], logs[:, 0, :], ACT.Exp, scale=-1.0)
        ratio = tile([P, PACK], F32, "ratio")
        nc.gpsimd.tensor_tensor(ratio[:], parts[:, 0, :], inverse[:], ALU.mult)
        fix = tile([P, PACK], F32, "fix")
        nc.gpsimd.tensor_scalar(fix[:], ratio[:], -1.0, ln_c[:], ALU.add, ALU.add)
        outer = tile([P, PACK], F32, "outer")
        nc.gpsimd.tensor_tensor(outer[:], logs[:, 1, :], logs[:, 2, :], ALU.add)
        fixed = tile([P, PACK], F32, "fixed")
        nc.gpsimd.tensor_tensor(fixed[:], fix[:], outer[:], ALU.add)
        ln_unit = tile([P, PACK], F32, "ln_unit")
        nc.gpsimd.tensor_tensor(ln_unit[:], fixed[:], logs[:, 0, :], ALU.add)

        picked_rows = keep.tile([P, S], U8, name="picked_rows", tag="late", align_bytes=64)
        nc.vector.tensor_copy(picked_rows[:], scale_rows[:].indirect(offsets[:]))
        for q in range(4):
            nc.scalar.dma_start(
                x_plane[32 * q : 32 * q + 4, :].bitcast(I32),
                picked_rows[32 * q : 32 * q + 32 : 8, :].bitcast(I32),
            )
        late = keep.tile([P, PACK * N + S], F32, name="late", tag="late", align_bytes=64)
        wo_raw = late[:, 0 : PACK * N]
        skip_sb = late[:, PACK * N : PACK * N + S]
        nc.sync.dma_start(wo_raw, wo.rearrange("(p j) m -> p (j m)", j=PACK))
        nc.sync.dma_start(skip_sb, skip)
        x_codes = []
        for h in range(2):
            picked = tile([P, HALF], U32, "picked%d" % h)
            nc.vector.tensor_copy(
                picked[:], words[:].bitcast(U32).indirect(offsets[:, h * 32 : (h + 1) * 32])
            )
            x_codes.append(picked)

        w1_codes, w1_planes = [], []
        grouped = [tile([P, 2, P, PACK], BF16, "w1_grouped%d" % u) for u in range(2)]
        w1_src = w1_raw[:].rearrange("p j (m t) -> p m j t", t=PACK)
        for u, copy in enumerate((nc.vector.tensor_copy, nc.scalar.copy)):
            copy(grouped[u][:].rearrange("p t m j -> p m j t"), w1_src[:, :, :, 2 * u : 2 * u + 2])
        for t in range(PACK):
            codes = tile([P, P], U32, "w1_codes%d" % t)
            plane = tile([P, P], U8, "w1_plane%d" % t)
            nc.vector.quantize_mx(
                out=codes[:].bitcast(FP8X4),
                scales=plane[:],
                in_=grouped[t // 2][:, t % 2, :, :].rearrange("p m j -> p (m j)"),
            )
            w1_codes.append(codes)
            w1_planes.append(plane)

        def product(dst, t, h, lo, hi, start, stop):
            nc.tensor.matmul_mx(
                out=dst,
                lhsT=w1_codes[t][:].bitcast(FP8X4),
                lhsT_scale=w1_planes[t][:],
                rhs=x_codes[h][:, lo:hi].bitcast(FP8X4),
                rhs_scale=x_plane[:, h * HALF + lo : h * HALF + hi],
                start=start,
                stop=stop,
            )

        half_ln = -0.5 * math.log(0.8)
        biases = tile([P, 2, PACK], F32, "biases")
        folded = psum.tile([P, HALF], F32, name="bank7")
        summed = [t for t in range(PACK) if t != FOLDED]
        ys = {t: tile([P, S], F32, "y%d" % t) for t in summed}
        banks, totals = {}, {}

        def whole_half(t, h):
            banks[t, h] = psum.tile([P, HALF], F32, name="bank%d" % (2 * t + h))
            product(banks[t, h][:], t, h, 0, HALF, True, True)

        def fold_half(h):
            for lo in range(0, HALF, FOLD):
                product(folded[:, 0:FOLD], FOLDED, h, lo, lo + FOLD, (h, lo) == (0, 0), (h, lo) == (1, HALF - FOLD))

        def exp_bias(t):
            nc.vector.tensor_scalar(
                biases[:, 1, t : t + 1], biases[:, 0, t : t + 1], -2.0, ln_unit[:, t : t + 1], ALU.mult, ALU.add
            )

        def first_half(t):
            whole_half(t, 0)
            totals[t] = tile([P, 1], F32, "total%d" % t)
            if t in SCALAR_SUMS:
                bare = tile([P, 1], F32, "bare%d" % t)
                nc.scalar.activation(ys[t][:, 0:HALF], banks[t, 0][:], ACT.Copy, scale=Y_SCALE, accum_out=bare[:])
                nc.scalar.activation(totals[t][:], bare[:], ACT.Copy, bias=half_ln)
            else:
                nc.vector.tensor_scalar(
                    ys[t][:, 0:HALF], banks[t, 0][:], Y_SCALE, half_ln, ALU.mult, ALU.add, accum_out=totals[t][:]
                )

        def second_half(t):
            whole_half(t, 1)
            nc.vector.tensor_scalar(
                ys[t][:, HALF:S], banks[t, 1][:], Y_SCALE, totals[t][:], ALU.mult, ALU.add,
                accum_out=biases[:, 0, t : t + 1],
            )
            exp_bias(t)

        first_half(0)
        first_half(2)
        second_half(0)
        fold_half(0)
        fold_half(1)
        row_sum = tile([P, 1], F32, "row_sum")
        nc.vector.tensor_reduce(row_sum[:], folded[:, 0:FOLD], mybir.AxisListType.X, ALU.add)
        nc.vector.tensor_scalar(biases[:, 0, FOLDED : FOLDED + 1], row_sum[:], Y_SCALE, half_ln, ALU.mult, ALU.add)
        exp_bias(FOLDED)
        whole_half(FOLDED, 0)
        first_half(3)
        second_half(2)
        second_half(3)
        whole_half(FOLDED, 1)
        late_biases = tile([P, 2, PACK], F32, "late_biases")
        nc.vector.tensor_copy(late_biases[:], biases[:])

        wo_signed = tile([P, PACK, N], BF16, "wo_signed")
        for j in range(PACK):
            nc.gpsimd.tensor_scalar(
                wo_signed[:, j, :], wo_raw[:, j * N : (j + 1) * N], sgn[:, j : j + 1], 0.0, ALU.mult, ALU.add
            )
        wo_grouped = tile([P, N, PACK], BF16, "wo_grouped")
        nc.vector.tensor_copy(
            wo_grouped[:].rearrange("p (c i) j -> p c j i", i=4),
            wo_signed[:].rearrange("p j (c i) -> p c j i", i=4),
        )
        wo_codes = tile([P, N], U32, "wo_codes")
        wo_plane = tile([P, N], U8, "wo_plane")
        nc.vector.quantize_mx(
            out=wo_codes[:].bitcast(FP8X4), scales=wo_plane[:], in_=wo_grouped[:].rearrange("p m j -> p (m j)")
        )

        th = tile([P, S // 4, PACK, 4], F32, "th")
        ex = tile([P, S // 4, PACK, 4], F32, "ex")

        def activate(t, a, b):
            if t == FOLDED:
                src, back = banks[t, a // HALF][:, a % HALF : a % HALF + b - a], 1.0
            else:
                src, back = ys[t][:, a:b], 1.0 / Y_SCALE
            src = src.rearrange("p (r i) -> p r i", i=4)
            rows = slice(a // 4, b // 4)
            shifts = late_biases if a else biases
            nc.scalar.activation(th[:, rows, t, :], src, ACT.Tanh, bias=shifts[:, 0, t : t + 1], scale=-0.5 * back)
            nc.scalar.activation(ex[:, rows, t, :], src, ACT.Exp, bias=shifts[:, 1, t : t + 1], scale=back)

        def combine(a, b):
            rows = slice(a // 4, b // 4)
            zz = tile([P, 4, (b - a) // 4, PACK], BF16, "zz%d" % a)
            nc.vector.scalar_tensor_tensor(
                zz[:].rearrange("p i r t -> p (r t) i"),
                th[:, rows, :, :].rearrange("p r t i -> p (r t) i"),
                0.575 / 0.425,
                ex[:, rows, :, :].rearrange("p r t i -> p (r t) i"),
                ALU.add,
                ALU.mult,
            )
            return zz[:].rearrange("p i r t -> p (i r t)")

        free_banks = [0, 1, 4, 5, 6, 7]

        def read_out(first, zz_flat, pieces):
            acc = psum.tile([P, HALF], F32, name="bank%d" % free_banks.pop(0))
            at = 0
            for piece in pieces:
                zz_codes = tile([P, piece], U32, "zz_codes%d" % (first + at))
                zz_plane = tile([P, piece], U8, "zz_plane%d" % (first + at))
                nc.vector.quantize_mx(
                    out=zz_codes[:].bitcast(FP8X4),
                    scales=zz_plane[:],
                    in_=zz_flat[:, PACK * at : PACK * (at + piece)],
                )
                nc.tensor.matmul_mx(
                    out=acc[:, at : at + piece],
                    lhsT=wo_codes[:].bitcast(FP8X4),
                    lhsT_scale=wo_plane[:],
                    rhs=zz_codes[:].bitcast(FP8X4),
                    rhs_scale=zz_plane[:],
                    start=True,
                    stop=True,
                )
                at += piece
            cols = slice(first, first + at)
            result = tile([P, at], F32, "result%d" % first)
            nc.vector.tensor_tensor(
                result[:].rearrange("p (r i) -> p r i", i=4),
                acc[:, 0:at].rearrange("p (i r) -> p r i", i=4),
                skip_sb[:, cols].rearrange("p (r i) -> p r i", i=4),
                ALU.add,
            )
            nc.sync.dma_start(out[:, cols], result[:])

        done = [0] * PACK
        first = 0
        for pieces in CHUNKS:
            last = first + sum(pieces)
            for t in range(PACK):
                if done[t] < last:
                    reach = max(last, LEADS[t])
                    activate(t, done[t], reach)
                    done[t] = reach
            read_out(first, combine(first, last), pieces)
            first = last
